import numpy as np
import ml_dtypes


def mxq(x, axis, fmt="e4m3"):
    dtype, down = {"e4m3": (ml_dtypes.float8_e4m3fn, 7), "e5m2": (ml_dtypes.float8_e5m2, 14)}[fmt]
    v = np.moveaxis(np.asarray(x, np.float32).astype(ml_dtypes.bfloat16).astype(np.float64), axis, -1)
    blocks = v.reshape(v.shape[:-1] + (-1, 32))
    amax = np.abs(blocks).max(-1, keepdims=True)
    byte = np.maximum(np.where(amax > 0, np.frexp(amax)[1] - 1 + 127, 0) - down, 1)
    scale = np.exp2(byte - 127.0)
    codes = (blocks / scale).astype(np.float32).astype(dtype).astype(np.float64)
    return np.moveaxis((codes * scale).reshape(v.shape), -1, axis)


WIDE = False


def mx_kscale(k):
    if not WIDE:
        return np.ones(k)
    levels = np.array([10, -10, 5, -5, 0])
    if k % 512:
        return np.exp2(np.random.permutation(np.resize(levels, k // 32))).repeat(32)
    a = np.empty((k // 512, 16))
    for p in range(k // 512):
        a[p, :8] = np.random.permutation(np.resize(levels, 8))
        for g in range(8):
            far = levels[np.abs(levels - a[p, g]) >= 10]
            a[p, g + 8] = far[np.random.randint(len(far))]
    return np.exp2(a.ravel()).repeat(32)


BF16 = ml_dtypes.bfloat16


def bf(x):
    return np.asarray(x, np.float32).astype(BF16)


def f64(x):
    return np.asarray(x).astype(np.float64)


M, K, R, U, B = 1536, 1024, 512, 1024, 1024


def setup_inputs():
    s = mx_kscale(K)
    u = mx_kscale(M)
    size = np.exp(0.4 * np.random.standard_normal((B, 1)))
    return {"x": bf(np.random.standard_normal((M, K)) * s * u[:, None]),
            "cov_factor": bf(np.random.standard_normal((K, R)) / np.sqrt(K) / s[:, None]),
            "theta": bf(np.random.standard_normal((K, U)) / np.sqrt(K) / s[:, None]),
            "pop": bf(0.5 * np.random.standard_normal(M) * u),
            "cold": bf(np.exp(0.3 * np.random.standard_normal(M))),
            "slates": bf(np.random.standard_normal((B, M)) * size / np.sqrt(M) / u),
            "floor_sd": bf(0.5 + 0.5 * np.random.random_sample(B)),
            "alpha": bf(0.5 + np.random.random_sample(U))}


def reference(x, cov_factor, theta, pop, cold, slates, floor_sd, alpha):
    xq = mxq(f64(x), 1, "e4m3")
    sq = mxq(f64(slates), 1, "e4m3")
    h = (xq @ mxq(f64(cov_factor), 0, "e4m3")) * f64(cold)[:, None]
    v = np.maximum((xq @ mxq(f64(theta), 0, "e4m3")) + f64(pop)[:, None], 0.0)
    e = sq @ mxq(h, 0, "e4m3")
    mean = sq @ mxq(v, 0, "e4m3")
    width = np.sqrt(np.square(f64(floor_sd)) + np.mean(np.square(e), axis=1))
    ucb = mean + width[:, None] * f64(alpha)[None, :]
    return ucb, width

@@ -1,0 +1,262 @@
+from contextlib import ExitStack
+
+import concourse.mybir as mybir
+from concourse.masks import make_identity
+
+F32 = mybir.dt.float32
+BF16 = mybir.dt.bfloat16
+U32 = mybir.dt.uint32
+U8 = mybir.dt.uint8
+FP8X4 = mybir.dt.float8_e4m3fn_x4
+ACT = mybir.ActivationFunctionType
+ALU = mybir.AluOpType
+
+P = 128
+PACK = 4
+K_PASS = P * PACK
+N_TILE = 512
+
+ITEMS, FEATURES, RANK, USERS, SLATES = 1536, 1024, 512, 1024, 1024
+
+FLOPS = 2 * ITEMS * FEATURES * (RANK + USERS) + 2 * SLATES * ITEMS * (RANK + USERS)
+
+GROUPS = ITEMS // K_PASS
+F_PASSES = FEATURES // K_PASS
+B_TILES = SLATES // P
+
+MANUAL = True
+W_COPY = {}
+EXITS = {}
+LOADS = [("X", 0, 0), ("X", 0, 1), ("W", 0, 0), ("W", 0, 1), ("cold",), ("X", 1, 0), ("X", 1, 1), ("W", 1, 0), ("X", 2, 0), ("X", 2, 1), ("pop",), ("W", 1, 1), ("S", 0), ("S", 1), ("W", 2, 0), ("W", 2, 1), ("S", 2), ("S", 3)]
+PROGRAM = (
+    [("X", 0, 0), ("X", 0, 1), ("W", 0, 0), ("W", 0, 1), ("X", 1, 0), ("X", 1, 1), ("A", 0, 0), ("W", 1, 0), ("X", 2, 0), ("X", 2, 1), ("A", 0, 1), ("W", 1, 1), ("A", 0, 2), ("S", 0), ("A", 1, 0), ("S", 1), ("A", 1, 1)]
+    + [("B", 0, 0), ("W", 2, 0), ("S", 2), ("B", 0, 1), ("W", 2, 1), ("A", 1, 2), ("S", 3), ("B", 0, 2), ("A", 2, 0), ("B", 0, 3), ("B", 0, 4), ("A", 2, 1), ("B", 0, 5), ("B", 0, 6), ("A", 2, 2), ("B", 0, 7), ("width",)]
+    + [("B", 1, b) for b in range(8)] + [("B", 2, b) for b in range(8)]
+)
+
+
+def tile_slate_clipped_payoff_ucb_f4_kernel(
+    tc, x, cov_factor, theta, pop, cold, slates, floor_sd, alpha, ucb, width
+):
+    nc = tc.nc
+    with ExitStack() as ctx:
+        keep = ctx.enter_context(tc.tile_pool(name="keep", bufs=1))
+        work = ctx.enter_context(tc.tile_pool(name="work", bufs=3))
+        psum = ctx.enter_context(tc.psum_pool(name="psum", bufs=8))
+        if MANUAL:
+            ctx.enter_context(tc.manual_schedule())
+
+        x_sb = [keep.tile([P, PACK, FEATURES], BF16, name="x_sb%d" % g, align_bytes=64) for g in range(GROUPS)]
+        s_sb = [keep.tile([P, 2, ITEMS], BF16, name="s_sb%d" % q, align_bytes=64) for q in range(B_TILES // 2)]
+        cov_sb = [keep.tile([P, PACK, RANK], BF16, name="cov_sb%d" % f, align_bytes=64) for f in range(F_PASSES)]
+        theta_sb = [keep.tile([P, PACK, USERS], BF16, name="theta_sb%d" % f, align_bytes=64) for f in range(F_PASSES)]
+        x_codes = [[keep.tile([P, F_PASSES, 256], U32, name="x_codes%d_%d" % (g, h), align_bytes=64) for h in range(2)] for g in range(GROUPS)]
+        x_scales = [[keep.tile([P, F_PASSES, 256], U8, name="x_scales%d_%d" % (g, h), align_bytes=64) for h in range(2)] for g in range(GROUPS)]
+        s_codes = [keep.tile([P, GROUPS, 256], U32, name="s_codes%d" % q, align_bytes=64) for q in range(B_TILES // 2)]
+        s_scales = [keep.tile([P, GROUPS, 256], U8, name="s_scales%d" % q, align_bytes=64) for q in range(B_TILES // 2)]
+        w_codes = [[keep.tile([P, N_TILE], U32, name="w_codes%d_%d" % (c, f), align_bytes=64) for f in range(F_PASSES)] for c in range(3)]
+        w_scales = [[keep.tile([P, N_TILE], U8, name="w_scales%d_%d" % (c, f), align_bytes=64) for f in range(F_PASSES)] for c in range(3)]
+        r_codes = [[keep.tile([P, N_TILE], U32, name="r_codes%d_%d" % (c, g), align_bytes=64) for g in range(GROUPS)] for c in range(3)]
+        r_scales = [[keep.tile([P, N_TILE], U8, name="r_scales%d_%d" % (c, g), align_bytes=64) for g in range(GROUPS)] for c in range(3)]
+        ident = keep.tile([P, P], F32, name="ident")
+        cold_bf = keep.tile([P, GROUPS, PACK], BF16, name="cold_bf")
+        pop_bf = keep.tile([P, GROUPS, PACK], BF16, name="pop_bf")
+        cold_col = keep.tile([P, GROUPS, PACK], F32, name="cold_col")
+        pop_col = keep.tile([P, GROUPS, PACK], F32, name="pop_col")
+        floor_bf = keep.tile([P, B_TILES], BF16, name="floor_bf")
+        floor_sq = keep.tile([P, B_TILES], F32, name="floor_sq")
+        alpha_bf = keep.tile([P, USERS], BF16, name="alpha_bf")
+        e_sq = keep.tile([P, B_TILES], F32, name="e_sq")
+        var = keep.tile([P, B_TILES], F32, name="var")
+        width_col = keep.tile([P, B_TILES], F32, name="width_col")
+        warm = keep.tile([P, 1], F32, name="warm")
+
+        x_rows = x.rearrange("(g p t) k -> g p t k", p=P, t=PACK)
+        s_rows = slates.rearrange("(p b) k -> p b k", b=B_TILES)
+        def load_x(g, h):
+            nc.sync.dma_start(out=x_sb[g][:, 2 * h : 2 * h + 2, :], in_=x_rows[g, :, 2 * h : 2 * h + 2, :])
+        def load_s(q):
+            nc.sync.dma_start(out=s_sb[q][:], in_=s_rows[:, 2 * q : 2 * q + 2, :])
+        make_identity(nc, ident[:])
+        nc.vector.memset(warm[:], 1.0)
+        nc.scalar.activation(out=warm[:], in_=warm[:], func=ACT.Sqrt)
+
+        def load_w(c, f):
+            rows = slice(f * K_PASS, (f + 1) * K_PASS)
+            if c == 0:
+                dst, src = cov_sb[f][:], cov_factor[rows, :]
+            else:
+                cols = slice((c - 1) * N_TILE, c * N_TILE)
+                dst, src = theta_sb[f][:, :, cols], theta[rows, cols]
+            nc.sync.dma_start(out=dst, in_=src.rearrange("(p j) n -> p j n", j=PACK))
+
+        def load_cold():
+            nc.sync.dma_start(out=cold_bf[:], in_=cold.rearrange("(g p t) -> p g t", p=P, t=PACK))
+
+        def load_pop():
+            nc.sync.dma_start(out=pop_bf[:], in_=pop.rearrange("(g p t) -> p g t", p=P, t=PACK))
+
+        loader = {"X": load_x, "S": load_s, "W": load_w, "cold": load_cold, "pop": load_pop}
+        for load in LOADS:
+            loader[load[0]](*load[1:])
+        nc.sync.dma_start(out=floor_bf[:], in_=floor_sd.rearrange("(p b) -> p b", b=B_TILES))
+        nc.sync.dma_start(out=alpha_bf[:], in_=alpha.partition_broadcast(P))
+
+        def interleave(engine_copy, dst, src):
+            engine_copy(
+                out=dst.rearrange("p (c i) t -> p c t i", i=4),
+                in_=src.rearrange("p t (c i) -> p c t i", i=4),
+            )
+
+        def quantize(codes, scales, grouped):
+            nc.vector.quantize_mx(out=codes.bitcast(FP8X4), scales=scales, in_=grouped)
+
+        def turn(banks, words, passes):
+            for f in range(passes):
+                for a in range(2):
+                    for u in range(2):
+                        nc.tensor.transpose(
+                            banks[f][:, u, a * P : (a + 1) * P],
+                            words[:, a, 256 * f + u : 256 * (f + 1) : 2],
+                            ident[:],
+                        )
+
+        def x_job(g, h):
+            st = {}
+            def t0():
+                st["banks"] = [psum.tile([P, 2, 256], F32, name="bank") for f in range(F_PASSES)]
+                words = x_sb[g][:, 2 * h : 2 * h + 2, :].rearrange("p t k -> p (t k)").bitcast(F32).rearrange("p (t k) -> p t k", t=2)
+                turn(st["banks"], words, F_PASSES)
+            def t1():
+                st["grouped"] = work.tile([P, F_PASSES * 256 * PACK], BF16, name="turned_x", align_bytes=64)
+                gw = st["grouped"][:].bitcast(F32).rearrange("p (f w u) -> p f w u", f=F_PASSES, u=2)
+                for f in range(F_PASSES):
+                    eng = EXITS.get(("X", g, h), "SS")[f]
+                    src = st["banks"][f][:].rearrange("p u w -> p w u")
+                    if eng == "S":
+                        nc.scalar.copy(out=gw[:, f, :, :], in_=src)
+                    else:
+                        nc.vector.tensor_copy(out=gw[:, f, :, :], in_=src)
+            def t2():
+                quantize(x_codes[g][h][:].rearrange("p f w -> p (f w)"), x_scales[g][h][:].rearrange("p f w -> p (f w)"), st["grouped"][:])
+            return [t0, t1, t2]
+
+        def s_job(q):
+            st = {}
+            def t0():
+                st["banks"] = [psum.tile([P, 2, 256], F32, name="bank") for f in range(GROUPS)]
+                words = s_sb[q][:].rearrange("p t k -> p (t k)").bitcast(F32).rearrange("p (t k) -> p t k", t=2)
+                turn(st["banks"], words, GROUPS)
+            def t1():
+                st["grouped"] = work.tile([P, GROUPS * 256 * PACK], BF16, name="turned_s", align_bytes=64)
+                gw = st["grouped"][:].bitcast(F32).rearrange("p (f w u) -> p f w u", f=GROUPS, u=2)
+                for f in range(GROUPS):
+                    eng = EXITS.get(("S", q), "SSS")[f]
+                    src = st["banks"][f][:].rearrange("p u w -> p w u")
+                    if eng == "S":
+                        nc.scalar.copy(out=gw[:, f, :, :], in_=src)
+                    else:
+                        nc.vector.tensor_copy(out=gw[:, f, :, :], in_=src)
+            def t2():
+                codes = s_codes[q][:].rearrange("p f w -> p (f w)")
+                scales = s_scales[q][:].rearrange("p f w -> p (f w)")
+                quantize(codes[:, :512], scales[:, :512], st["grouped"][:, :2048])
+                quantize(codes[:, 512:], scales[:, 512:], st["grouped"][:, 2048:])
+            return [t0, t1, t2]
+
+        def w_job(c, f):
+            st = {}
+            def t0():
+                src = cov_sb[f][:] if c == 0 else theta_sb[f][:, :, (c - 1) * N_TILE : c * N_TILE]
+                st["grouped"] = work.tile([P, N_TILE, PACK], BF16, name="grouped_w", align_bytes=64)
+                copy = nc.scalar.copy if W_COPY.get((c, f), "V") == "S" else nc.vector.tensor_copy
+                interleave(copy, st["grouped"][:], src)
+            def t1():
+                quantize(w_codes[c][f][:], w_scales[c][f][:], st["grouped"][:].rearrange("p n t -> p (n t)"))
+            return [t0, t1]
+
+        def a_job(c, g):
+            st = {}
+            def t0():
+                st["banks"] = []
+                for t in range(PACK):
+                    bank = psum.tile([P, N_TILE], F32, name="bank")
+                    for f in range(F_PASSES):
+                        cols = slice((t % 2) * P, (t % 2 + 1) * P)
+                        nc.tensor.matmul_mx(
+                            out=bank[:],
+                            lhsT=x_codes[g][t // 2][:, f, cols].bitcast(FP8X4),
+                            lhsT_scale=x_scales[g][t // 2][:, f, cols],
+                            rhs=w_codes[c][f][:].bitcast(FP8X4),
+                            rhs_scale=w_scales[c][f][:],
+                            start=(f == 0),
+                            stop=(f == F_PASSES - 1),
+                        )
+                    st["banks"].append(bank)
+            def t1():
+                if (c, g) == (0, 0):
+                    nc.vector.tensor_copy(out=cold_col[:], in_=cold_bf[:])
+                if (c, g) == (1, 0):
+                    nc.vector.tensor_copy(out=pop_col[:], in_=pop_bf[:])
+                st["rows"] = work.tile([P, PACK, N_TILE], BF16, name="rows", align_bytes=64)
+                for t in range(PACK):
+                    bank = st["banks"][t]
+                    if c == 0:
+                        if EXITS.get(("A", c, g), "SSSS")[t] == "S":
+                            nc.scalar.activation(out=st["rows"][:, t, :], in_=bank[:], func=ACT.Copy, scale=cold_col[:, g, t : t + 1])
+                        else:
+                            nc.vector.tensor_scalar(out=st["rows"][:, t, :], in0=bank[:], scalar1=cold_col[:, g, t : t + 1], scalar2=None, op0=ALU.mult)
+                    else:
+                        if EXITS.get(("A", c, g), "SSSS")[t] == "S":
+                            nc.scalar.activation(out=st["rows"][:, t, :], in_=bank[:], func=ACT.Relu, bias=pop_col[:, g, t : t + 1])
+                        else:
+                            nc.vector.tensor_scalar(out=st["rows"][:, t, :], in0=bank[:], scalar1=pop_col[:, g, t : t + 1], scalar2=0.0, op0=ALU.add, op1=ALU.max)
+            def t2():
+                st["grouped"] = work.tile([P, N_TILE, PACK], BF16, name="grouped_r", align_bytes=64)
+                interleave(nc.vector.tensor_copy, st["grouped"][:], st["rows"][:])
+            def t3():
+                quantize(r_codes[c][g][:], r_scales[c][g][:], st["grouped"][:].rearrange("p n t -> p (n t)"))
+            return [t0, t1, t2, t3]
+
+        def b_job(c, b):
+            st = {}
+            def t0():
+                st["bank"] = psum.tile([P, N_TILE], F32, name="bank")
+                cols = slice((b % 2) * P, (b % 2 + 1) * P)
+                for g in range(GROUPS):
+                    nc.tensor.matmul_mx(
+                        out=st["bank"][:],
+                        lhsT=s_codes[b // 2][:, g, cols].bitcast(FP8X4),
+                        lhsT_scale=s_scales[b // 2][:, g, cols],
+                        rhs=r_codes[c][g][:].bitcast(FP8X4),
+                        rhs_scale=r_scales[c][g][:],
+                        start=(g == 0),
+                        stop=(g == GROUPS - 1),
+                    )
+            def t1():
+                if c == 0:
+                    junk = work.tile([P, N_TILE], F32, name="junk")
+                    nc.scalar.activation(out=junk[:], in_=st["bank"][:], func=ACT.Square, accum_out=e_sq[:, b : b + 1])
+                else:
+                    cols = slice((c - 1) * N_TILE, c * N_TILE)
+                    res = work.tile([P, N_TILE], F32, name="res", bufs=4)
+                    nc.vector.scalar_tensor_tensor(
+                        out=res[:], in0=alpha_bf[:, cols], scalar=width_col[:, b : b + 1], in1=st["bank"][:], op0=ALU.mult, op1=ALU.add,
+                    )
+                    nc.sync.dma_start(out=ucb.rearrange("(p b) n -> p b n", b=B_TILES)[:, b, cols], in_=res[:])
+            return [t0, t1]
+
+        def width_job():
+            def t0():
+                nc.vector.tensor_tensor(out=floor_sq[:], in0=floor_bf[:], in1=floor_bf[:], op=ALU.mult)
+                nc.vector.scalar_tensor_tensor(out=var[:], in0=e_sq[:], scalar=1.0 / RANK, in1=floor_sq[:], op0=ALU.mult, op1=ALU.add)
+                nc.scalar.activation(out=width_col[:], in_=var[:], func=ACT.Sqrt)
+                nc.sync.dma_start(out=width.rearrange("(p b) -> p b", b=B_TILES), in_=width_col[:])
+            return [t0]
+
+        make = {"X": x_job, "S": s_job, "W": w_job, "A": a_job, "B": b_job, "width": width_job}
+        jobs = [make[step[0]](*step[1:]) for step in PROGRAM]
+        for i in range(len(jobs) + 3):
+            for s in (3, 2, 1, 0):
+                if 0 <= i - s < len(jobs) and s < len(jobs[i - s]):
+                    jobs[i - s][s]()

@@ -24,13 +24,15 @@ GROUPS = ITEMS // K_PASS
 F_PASSES = FEATURES // K_PASS
 B_TILES = SLATES // P
 
-MANUAL = True
 W_COPY = {}
 EXITS = {}
-LOADS = [("X", 0, 0), ("X", 0, 1), ("W", 0, 0), ("W", 0, 1), ("cold",), ("X", 1, 0), ("X", 1, 1), ("W", 1, 0), ("X", 2, 0), ("X", 2, 1), ("pop",), ("W", 1, 1), ("S", 0), ("S", 1), ("W", 2, 0), ("W", 2, 1), ("S", 2), ("S", 3)]
+WARM = {}
+COLS_AT = 8
+MANUAL = True
+LOADS = [("X", 0, 0), ("X", 0, 1), ("W", 0, 0), ("W", 0, 1), ("X", 1, 0), ("X", 1, 1), ("X", 2, 0), ("X", 2, 1), ("S", 0), ("W", 1, 0), ("W", 1, 1), ("S", 1), ("S", 2), ("S", 3), ("W", 2, 0), ("W", 2, 1)]
 PROGRAM = (
-    [("X", 0, 0), ("X", 0, 1), ("W", 0, 0), ("W", 0, 1), ("X", 1, 0), ("X", 1, 1), ("A", 0, 0), ("W", 1, 0), ("X", 2, 0), ("X", 2, 1), ("A", 0, 1), ("W", 1, 1), ("A", 0, 2), ("S", 0), ("A", 1, 0), ("S", 1), ("A", 1, 1)]
-    + [("B", 0, 0), ("W", 2, 0), ("S", 2), ("B", 0, 1), ("W", 2, 1), ("A", 1, 2), ("S", 3), ("B", 0, 2), ("A", 2, 0), ("B", 0, 3), ("B", 0, 4), ("A", 2, 1), ("B", 0, 5), ("B", 0, 6), ("A", 2, 2), ("B", 0, 7), ("width",)]
+    [("X", 0, 0), ("X", 0, 1), ("W", 0, 0), ("W", 0, 1), ("X", 1, 0), ("X", 1, 1), ("X", 2, 0), ("X", 2, 1), ("A", 0, 0), ("S", 0), ("W", 1, 0), ("W", 1, 1), ("A", 0, 1), ("S", 1), ("A", 0, 2), ("S", 2), ("A", 1, 0), ("S", 3), ("W", 2, 0), ("B", 0, 0), ("W", 2, 1), ("A", 1, 1)]
+    + [("B", 0, b) for b in range(1, 4)] + [("A", 1, 2)] + [("B", 0, b) for b in range(4, 8)] + [("A", 2, g) for g in range(3)] + [("width",)]
     + [("B", 1, b) for b in range(8)] + [("B", 2, b) for b in range(8)]
 )
 
@@ -42,7 +44,7 @@ def tile_slate_clipped_payoff_ucb_f4_kernel(
     with ExitStack() as ctx:
         keep = ctx.enter_context(tc.tile_pool(name="keep", bufs=1))
         work = ctx.enter_context(tc.tile_pool(name="work", bufs=3))
-        psum = ctx.enter_context(tc.psum_pool(name="psum", bufs=8))
+        psum = ctx.enter_context(tc.psum_pool(name="psum", bufs=1))
         if MANUAL:
             ctx.enter_context(tc.manual_schedule())
 
@@ -59,10 +61,10 @@ def tile_slate_clipped_payoff_ucb_f4_kernel(
         r_codes = [[keep.tile([P, N_TILE], U32, name="r_codes%d_%d" % (c, g), align_bytes=64) for g in range(GROUPS)] for c in range(3)]
         r_scales = [[keep.tile([P, N_TILE], U8, name="r_scales%d_%d" % (c, g), align_bytes=64) for g in range(GROUPS)] for c in range(3)]
         ident = keep.tile([P, P], F32, name="ident")
-        cold_bf = keep.tile([P, GROUPS, PACK], BF16, name="cold_bf")
-        pop_bf = keep.tile([P, GROUPS, PACK], BF16, name="pop_bf")
-        cold_col = keep.tile([P, GROUPS, PACK], F32, name="cold_col")
-        pop_col = keep.tile([P, GROUPS, PACK], F32, name="pop_col")
+        item_rows = keep.tile([P, K_PASS], BF16, name="item_rows", align_bytes=64)
+        item_cols = keep.tile([P, PACK, 2 * GROUPS], F32, name="item_cols")
+        ident_bf = keep.tile([P, P], BF16, name="ident_bf")
+        zeros = keep.tile([P, N_TILE], BF16, name="zeros")
         floor_bf = keep.tile([P, B_TILES], BF16, name="floor_bf")
         floor_sq = keep.tile([P, B_TILES], F32, name="floor_sq")
         alpha_bf = keep.tile([P, USERS], BF16, name="alpha_bf")
@@ -77,7 +79,10 @@ def tile_slate_clipped_payoff_ucb_f4_kernel(
             nc.sync.dma_start(out=x_sb[g][:, 2 * h : 2 * h + 2, :], in_=x_rows[g, :, 2 * h : 2 * h + 2, :])
         def load_s(q):
             nc.sync.dma_start(out=s_sb[q][:], in_=s_rows[:, 2 * q : 2 * q + 2, :])
+        nc.vector.memset(item_rows[:], 0.0)
+        nc.vector.memset(zeros[:], 0.0)
         make_identity(nc, ident[:])
+        nc.vector.tensor_copy(out=ident_bf[:], in_=ident[:])
         nc.vector.memset(warm[:], 1.0)
         nc.scalar.activation(out=warm[:], in_=warm[:], func=ACT.Sqrt)
 
@@ -90,17 +95,19 @@ def tile_slate_clipped_payoff_ucb_f4_kernel(
                 dst, src = theta_sb[f][:, :, cols], theta[rows, cols]
             nc.sync.dma_start(out=dst, in_=src.rearrange("(p j) n -> p j n", j=PACK))
 
-        def load_cold():
-            nc.sync.dma_start(out=cold_bf[:], in_=cold.rearrange("(g p t) -> p g t", p=P, t=PACK))
-
-        def load_pop():
-            nc.sync.dma_start(out=pop_bf[:], in_=pop.rearrange("(g p t) -> p g t", p=P, t=PACK))
-
-        loader = {"X": load_x, "S": load_s, "W": load_w, "cold": load_cold, "pop": load_pop}
+        nc.scalar.dma_start(out=item_rows[0:GROUPS, :], in_=cold.rearrange("(g n) -> g n", g=GROUPS))
+        nc.scalar.dma_start(out=item_rows[GROUPS : 2 * GROUPS, :], in_=pop.rearrange("(g n) -> g n", g=GROUPS))
+        loader = {"X": load_x, "S": load_s, "W": load_w}
         for load in LOADS:
             loader[load[0]](*load[1:])
         nc.sync.dma_start(out=floor_bf[:], in_=floor_sd.rearrange("(p b) -> p b", b=B_TILES))
         nc.sync.dma_start(out=alpha_bf[:], in_=alpha.partition_broadcast(P))
+
+        used = []
+
+        def next_bank(shape, dtype=F32):
+            used.append(len(used) % 8)
+            return psum.tile(shape, dtype, name="bank%d" % used[-1])
 
         def interleave(engine_copy, dst, src):
             engine_copy(
@@ -124,7 +131,7 @@ def tile_slate_clipped_payoff_ucb_f4_kernel(
         def x_job(g, h):
             st = {}
             def t0():
-                st["banks"] = [psum.tile([P, 2, 256], F32, name="bank") for f in range(F_PASSES)]
+                st["banks"] = [next_bank([P, 2, 256]) for f in range(F_PASSES)]
                 words = x_sb[g][:, 2 * h : 2 * h + 2, :].rearrange("p t k -> p (t k)").bitcast(F32).rearrange("p (t k) -> p t k", t=2)
                 turn(st["banks"], words, F_PASSES)
             def t1():
@@ -144,7 +151,7 @@ def tile_slate_clipped_payoff_ucb_f4_kernel(
         def s_job(q):
             st = {}
             def t0():
-                st["banks"] = [psum.tile([P, 2, 256], F32, name="bank") for f in range(GROUPS)]
+                st["banks"] = [next_bank([P, 2, 256]) for f in range(GROUPS)]
                 words = s_sb[q][:].rearrange("p t k -> p (t k)").bitcast(F32).rearrange("p (t k) -> p t k", t=2)
                 turn(st["banks"], words, GROUPS)
             def t1():
@@ -180,7 +187,7 @@ def tile_slate_clipped_payoff_ucb_f4_kernel(
             def t0():
                 st["banks"] = []
                 for t in range(PACK):
-                    bank = psum.tile([P, N_TILE], F32, name="bank")
+                    bank = next_bank([P, N_TILE])
                     for f in range(F_PASSES):
                         cols = slice((t % 2) * P, (t % 2 + 1) * P)
                         nc.tensor.matmul_mx(
@@ -194,23 +201,19 @@ def tile_slate_clipped_payoff_ucb_f4_kernel(
                         )
                     st["banks"].append(bank)
             def t1():
-                if (c, g) == (0, 0):
-                    nc.vector.tensor_copy(out=cold_col[:], in_=cold_bf[:])
-                if (c, g) == (1, 0):
-                    nc.vector.tensor_copy(out=pop_col[:], in_=pop_bf[:])
-                st["rows"] = work.tile([P, PACK, N_TILE], BF16, name="rows", align_bytes=64)
+                st["rows"] = work.tile([P, PACK, N_TILE], BF16, name="rows", align_bytes=64, bufs=4)
                 for t in range(PACK):
                     bank = st["banks"][t]
                     if c == 0:
                         if EXITS.get(("A", c, g), "SSSS")[t] == "S":
-                            nc.scalar.activation(out=st["rows"][:, t, :], in_=bank[:], func=ACT.Copy, scale=cold_col[:, g, t : t + 1])
+                            nc.scalar.activation(out=st["rows"][:, t, :], in_=bank[:], func=ACT.Copy, scale=item_cols[:, t, g : g + 1])
                         else:
-                            nc.vector.tensor_scalar(out=st["rows"][:, t, :], in0=bank[:], scalar1=cold_col[:, g, t : t + 1], scalar2=None, op0=ALU.mult)
+                            nc.vector.tensor_scalar(out=st["rows"][:, t, :], in0=bank[:], scalar1=item_cols[:, t, g : g + 1], scalar2=None, op0=ALU.mult)
                     else:
                         if EXITS.get(("A", c, g), "SSSS")[t] == "S":
-                            nc.scalar.activation(out=st["rows"][:, t, :], in_=bank[:], func=ACT.Relu, bias=pop_col[:, g, t : t + 1])
+                            nc.scalar.activation(out=st["rows"][:, t, :], in_=bank[:], func=ACT.Relu, bias=item_cols[:, t, GROUPS + g : GROUPS + g + 1])
                         else:
-                            nc.vector.tensor_scalar(out=st["rows"][:, t, :], in0=bank[:], scalar1=pop_col[:, g, t : t + 1], scalar2=0.0, op0=ALU.add, op1=ALU.max)
+                            nc.vector.tensor_scalar(out=st["rows"][:, t, :], in0=bank[:], scalar1=item_cols[:, t, GROUPS + g : GROUPS + g + 1], scalar2=0.0, op0=ALU.add, op1=ALU.max)
             def t2():
                 st["grouped"] = work.tile([P, N_TILE, PACK], BF16, name="grouped_r", align_bytes=64)
                 interleave(nc.vector.tensor_copy, st["grouped"][:], st["rows"][:])
@@ -221,7 +224,7 @@ def tile_slate_clipped_payoff_ucb_f4_kernel(
         def b_job(c, b):
             st = {}
             def t0():
-                st["bank"] = psum.tile([P, N_TILE], F32, name="bank")
+                st["bank"] = next_bank([P, N_TILE])
                 cols = slice((b % 2) * P, (b % 2 + 1) * P)
                 for g in range(GROUPS):
                     nc.tensor.matmul_mx(
@@ -235,11 +238,11 @@ def tile_slate_clipped_payoff_ucb_f4_kernel(
                     )
             def t1():
                 if c == 0:
-                    junk = work.tile([P, N_TILE], F32, name="junk")
+                    junk = work.tile([P, N_TILE], F32, name="junk", bufs=1)
                     nc.scalar.activation(out=junk[:], in_=st["bank"][:], func=ACT.Square, accum_out=e_sq[:, b : b + 1])
                 else:
                     cols = slice((c - 1) * N_TILE, c * N_TILE)
-                    res = work.tile([P, N_TILE], F32, name="res", bufs=4)
+                    res = work.tile([P, N_TILE], F32, name="res", bufs=8)
                     nc.vector.scalar_tensor_tensor(
                         out=res[:], in0=alpha_bf[:, cols], scalar=width_col[:, b : b + 1], in1=st["bank"][:], op0=ALU.mult, op1=ALU.add,
                     )
@@ -254,9 +257,25 @@ def tile_slate_clipped_payoff_ucb_f4_kernel(
                 nc.sync.dma_start(out=width.rearrange("(p b) -> p b", b=B_TILES), in_=width_col[:])
             return [t0]
 
+        def item_columns():
+            bank = next_bank([P, PACK, P], BF16)
+            for t in range(PACK):
+                nc.tensor.transpose(bank[:, t, :], item_rows[:, t::PACK], ident_bf[:])
+            nc.vector.tensor_copy(out=item_cols[:], in_=bank[:, :, 0 : 2 * GROUPS])
+
+        def warm_up(n):
+            if n:
+                bank = next_bank([P, N_TILE])
+                for i in range(n):
+                    nc.tensor.matmul(bank[:], lhsT=zeros[:, :P], rhs=zeros[:], start=True, stop=True)
+
         make = {"X": x_job, "S": s_job, "W": w_job, "A": a_job, "B": b_job, "width": width_job}
         jobs = [make[step[0]](*step[1:]) for step in PROGRAM]
         for i in range(len(jobs) + 3):
             for s in (3, 2, 1, 0):
                 if 0 <= i - s < len(jobs) and s < len(jobs[i - s]):
+                    if s == 0:
+                        warm_up(WARM.get(PROGRAM[i], 0))
+                    if s == 0 and i == COLS_AT:
+                        item_columns()
                     jobs[i - s][s]()

@@ -24,15 +24,16 @@ GROUPS = ITEMS // K_PASS
 F_PASSES = FEATURES // K_PASS
 B_TILES = SLATES // P
 
-W_COPY = {}
+W_COPY = {(0, 1): "S"}
 EXITS = {}
-WARM = {}
-COLS_AT = 8
+WARM = {("X", 0, 0): 4, ("X", 1, 0): 3}
+COLS_AT = 7
 MANUAL = True
-LOADS = [("X", 0, 0), ("X", 0, 1), ("W", 0, 0), ("W", 0, 1), ("X", 1, 0), ("X", 1, 1), ("X", 2, 0), ("X", 2, 1), ("S", 0), ("W", 1, 0), ("W", 1, 1), ("S", 1), ("S", 2), ("S", 3), ("W", 2, 0), ("W", 2, 1)]
+LOADS = [("X", 0, 0), ("X", 0, 1), ("items",), ("W", 0, 0), ("W", 0, 1), ("X", 1, 0), ("X", 1, 1), ("W", 1, 0), ("X", 2, 0), ("X", 2, 1), ("W", 1, 1), ("S", 0), ("S", 1), ("W", 2, 0), ("W", 2, 1), ("S", 2), ("S", 3)]
 PROGRAM = (
-    [("X", 0, 0), ("X", 0, 1), ("W", 0, 0), ("W", 0, 1), ("X", 1, 0), ("X", 1, 1), ("X", 2, 0), ("X", 2, 1), ("A", 0, 0), ("S", 0), ("W", 1, 0), ("W", 1, 1), ("A", 0, 1), ("S", 1), ("A", 0, 2), ("S", 2), ("A", 1, 0), ("S", 3), ("W", 2, 0), ("B", 0, 0), ("W", 2, 1), ("A", 1, 1)]
-    + [("B", 0, b) for b in range(1, 4)] + [("A", 1, 2)] + [("B", 0, b) for b in range(4, 8)] + [("A", 2, g) for g in range(3)] + [("width",)]
+    [("X", 0, 0), ("X", 0, 1), ("W", 0, 0), ("W", 0, 1), ("X", 1, 0), ("X", 1, 1), ("W", 1, 0), ("A", 0, 0), ("X", 2, 0), ("X", 2, 1), ("A", 0, 1), ("W", 1, 1), ("S", 0), ("A", 0, 2), ("S", 1), ("A", 1, 0)]
+    + [("S", 2), ("W", 2, 0), ("A", 1, 1), ("W", 2, 1), ("S", 3), ("B", 0, 0), ("B", 0, 1), ("A", 1, 2)] + [("B", 0, b) for b in range(2, 6)]
+    + [("A", 2, 0), ("B", 0, 6), ("A", 2, 1), ("B", 0, 7), ("A", 2, 2), ("width",)]
     + [("B", 1, b) for b in range(8)] + [("B", 2, b) for b in range(8)]
 )
 
@@ -50,8 +51,7 @@ def tile_slate_clipped_payoff_ucb_f4_kernel(
 
         x_sb = [keep.tile([P, PACK, FEATURES], BF16, name="x_sb%d" % g, align_bytes=64) for g in range(GROUPS)]
         s_sb = [keep.tile([P, 2, ITEMS], BF16, name="s_sb%d" % q, align_bytes=64) for q in range(B_TILES // 2)]
-        cov_sb = [keep.tile([P, PACK, RANK], BF16, name="cov_sb%d" % f, align_bytes=64) for f in range(F_PASSES)]
-        theta_sb = [keep.tile([P, PACK, USERS], BF16, name="theta_sb%d" % f, align_bytes=64) for f in range(F_PASSES)]
+        w_sb = [[keep.tile([P, PACK, N_TILE], BF16, name="w_sb%d_%d" % (c, f), align_bytes=64) for f in range(F_PASSES)] for c in range(3)]
         x_codes = [[keep.tile([P, F_PASSES, 256], U32, name="x_codes%d_%d" % (g, h), align_bytes=64) for h in range(2)] for g in range(GROUPS)]
         x_scales = [[keep.tile([P, F_PASSES, 256], U8, name="x_scales%d_%d" % (g, h), align_bytes=64) for h in range(2)] for g in range(GROUPS)]
         s_codes = [keep.tile([P, GROUPS, 256], U32, name="s_codes%d" % q, align_bytes=64) for q in range(B_TILES // 2)]
@@ -79,8 +79,8 @@ def tile_slate_clipped_payoff_ucb_f4_kernel(
             nc.sync.dma_start(out=x_sb[g][:, 2 * h : 2 * h + 2, :], in_=x_rows[g, :, 2 * h : 2 * h + 2, :])
         def load_s(q):
             nc.sync.dma_start(out=s_sb[q][:], in_=s_rows[:, 2 * q : 2 * q + 2, :])
-        nc.vector.memset(item_rows[:], 0.0)
         nc.vector.memset(zeros[:], 0.0)
+        nc.gpsimd.memset(item_rows[:], 0.0)
         make_identity(nc, ident[:])
         nc.vector.tensor_copy(out=ident_bf[:], in_=ident[:])
         nc.vector.memset(warm[:], 1.0)
@@ -89,15 +89,16 @@ def tile_slate_clipped_payoff_ucb_f4_kernel(
         def load_w(c, f):
             rows = slice(f * K_PASS, (f + 1) * K_PASS)
             if c == 0:
-                dst, src = cov_sb[f][:], cov_factor[rows, :]
+                src = cov_factor[rows, :]
             else:
-                cols = slice((c - 1) * N_TILE, c * N_TILE)
-                dst, src = theta_sb[f][:, :, cols], theta[rows, cols]
-            nc.sync.dma_start(out=dst, in_=src.rearrange("(p j) n -> p j n", j=PACK))
+                src = theta[rows, (c - 1) * N_TILE : c * N_TILE]
+            nc.sync.dma_start(out=w_sb[c][f][:], in_=src.rearrange("(p j) n -> p j n", j=PACK))
 
-        nc.scalar.dma_start(out=item_rows[0:GROUPS, :], in_=cold.rearrange("(g n) -> g n", g=GROUPS))
-        nc.scalar.dma_start(out=item_rows[GROUPS : 2 * GROUPS, :], in_=pop.rearrange("(g n) -> g n", g=GROUPS))
-        loader = {"X": load_x, "S": load_s, "W": load_w}
+        def load_items():
+            nc.sync.dma_start(out=item_rows[0:GROUPS, :], in_=cold.rearrange("(g n) -> g n", g=GROUPS))
+            nc.sync.dma_start(out=item_rows[GROUPS : 2 * GROUPS, :], in_=pop.rearrange("(g n) -> g n", g=GROUPS))
+
+        loader = {"X": load_x, "S": load_s, "W": load_w, "items": load_items}
         for load in LOADS:
             loader[load[0]](*load[1:])
         nc.sync.dma_start(out=floor_bf[:], in_=floor_sd.rearrange("(p b) -> p b", b=B_TILES))
@@ -174,7 +175,7 @@ def tile_slate_clipped_payoff_ucb_f4_kernel(
         def w_job(c, f):
             st = {}
             def t0():
-                src = cov_sb[f][:] if c == 0 else theta_sb[f][:, :, (c - 1) * N_TILE : c * N_TILE]
+                src = w_sb[c][f][:]
                 st["grouped"] = work.tile([P, N_TILE, PACK], BF16, name="grouped_w", align_bytes=64)
                 copy = nc.scalar.copy if W_COPY.get((c, f), "V") == "S" else nc.vector.tensor_copy
                 interleave(copy, st["grouped"][:], src)

@@ -27,13 +27,13 @@ B_TILES = SLATES // P
 W_COPY = {(0, 1): "S"}
 EXITS = {}
 WARM = {("X", 0, 0): 4, ("X", 1, 0): 3}
-COLS_AT = 7
+COLS_AT = 4
 MANUAL = True
 LOADS = [("X", 0, 0), ("X", 0, 1), ("items",), ("W", 0, 0), ("W", 0, 1), ("X", 1, 0), ("X", 1, 1), ("W", 1, 0), ("X", 2, 0), ("X", 2, 1), ("W", 1, 1), ("S", 0), ("S", 1), ("W", 2, 0), ("W", 2, 1), ("S", 2), ("S", 3)]
 PROGRAM = (
-    [("X", 0, 0), ("X", 0, 1), ("W", 0, 0), ("W", 0, 1), ("X", 1, 0), ("X", 1, 1), ("W", 1, 0), ("A", 0, 0), ("X", 2, 0), ("X", 2, 1), ("A", 0, 1), ("W", 1, 1), ("S", 0), ("A", 0, 2), ("S", 1), ("A", 1, 0)]
-    + [("S", 2), ("W", 2, 0), ("A", 1, 1), ("W", 2, 1), ("S", 3), ("B", 0, 0), ("B", 0, 1), ("A", 1, 2)] + [("B", 0, b) for b in range(2, 6)]
-    + [("A", 2, 0), ("B", 0, 6), ("A", 2, 1), ("B", 0, 7), ("A", 2, 2), ("width",)]
+    [("X", 0, 0), ("X", 0, 1), ("W", 0, 0), ("W", 0, 1), ("X", 1, 0), ("W", 1, 0), ("X", 1, 1), ("A", 0, 0), ("W", 1, 1), ("X", 2, 0), ("X", 2, 1), ("A", 0, 1), ("S", 0), ("W", 2, 0), ("A", 0, 2)]
+    + [("S", 1), ("W", 2, 1), ("A", 1, 0), ("S", 2), ("A", 1, 1), ("S", 3), ("B", 0, 0), ("A", 1, 2)]
+    + [("B", 0, 1), ("A", 2, 0), ("B", 0, 2), ("A", 2, 1), ("B", 0, 3), ("A", 2, 2)] + [("B", 0, b) for b in range(4, 8)] + [("width",)]
     + [("B", 1, b) for b in range(8)] + [("B", 2, b) for b in range(8)]
 )
 
@@ -224,30 +224,35 @@ def tile_slate_clipped_payoff_ucb_f4_kernel(
 
         def b_job(c, b):
             st = {}
+            parts = [slice(0, N_TILE)] if (c, b) != (2, B_TILES - 1) else [slice(0, N_TILE // 2), slice(N_TILE // 2, N_TILE)]
             def t0():
-                st["bank"] = next_bank([P, N_TILE])
+                st["banks"] = []
                 cols = slice((b % 2) * P, (b % 2 + 1) * P)
-                for g in range(GROUPS):
-                    nc.tensor.matmul_mx(
-                        out=st["bank"][:],
-                        lhsT=s_codes[b // 2][:, g, cols].bitcast(FP8X4),
-                        lhsT_scale=s_scales[b // 2][:, g, cols],
-                        rhs=r_codes[c][g][:].bitcast(FP8X4),
-                        rhs_scale=r_scales[c][g][:],
-                        start=(g == 0),
-                        stop=(g == GROUPS - 1),
-                    )
+                for part in parts:
+                    bank = next_bank([P, part.stop - part.start])
+                    for g in range(GROUPS):
+                        nc.tensor.matmul_mx(
+                            out=bank[:],
+                            lhsT=s_codes[b // 2][:, g, cols].bitcast(FP8X4),
+                            lhsT_scale=s_scales[b // 2][:, g, cols],
+                            rhs=r_codes[c][g][:, part].bitcast(FP8X4),
+                            rhs_scale=r_scales[c][g][:, part],
+                            start=(g == 0),
+                            stop=(g == GROUPS - 1),
+                        )
+                    st["banks"].append(bank)
             def t1():
                 if c == 0:
                     junk = work.tile([P, N_TILE], F32, name="junk", bufs=1)
-                    nc.scalar.activation(out=junk[:], in_=st["bank"][:], func=ACT.Square, accum_out=e_sq[:, b : b + 1])
+                    nc.scalar.activation(out=junk[:], in_=st["banks"][0][:], func=ACT.Square, accum_out=e_sq[:, b : b + 1])
                 else:
-                    cols = slice((c - 1) * N_TILE, c * N_TILE)
-                    res = work.tile([P, N_TILE], F32, name="res", bufs=8)
-                    nc.vector.scalar_tensor_tensor(
-                        out=res[:], in0=alpha_bf[:, cols], scalar=width_col[:, b : b + 1], in1=st["bank"][:], op0=ALU.mult, op1=ALU.add,
-                    )
-                    nc.sync.dma_start(out=ucb.rearrange("(p b) n -> p b n", b=B_TILES)[:, b, cols], in_=res[:])
+                    for bank, part in zip(st["banks"], parts):
+                        users = slice((c - 1) * N_TILE + part.start, (c - 1) * N_TILE + part.stop)
+                        res = work.tile([P, part.stop - part.start], F32, name="res", bufs=8)
+                        nc.vector.scalar_tensor_tensor(
+                            out=res[:], in0=alpha_bf[:, users], scalar=width_col[:, b : b + 1], in1=bank[:], op0=ALU.mult, op1=ALU.add,
+                        )
+                        nc.sync.dma_start(out=ucb.rearrange("(p b) n -> p b n", b=B_TILES)[:, b, users], in_=res[:])
             return [t0, t1]
 
         def width_job():

@@ -24,16 +24,15 @@ GROUPS = ITEMS // K_PASS
 F_PASSES = FEATURES // K_PASS
 B_TILES = SLATES // P
 
-W_COPY = {(0, 1): "S"}
+W_COPY = {}
 EXITS = {}
-WARM = {("X", 0, 0): 4, ("X", 1, 0): 3}
-COLS_AT = 4
+WARM = {("X", 0, 0): 4, ("X", 1, 0): 1, ("X", 1, 1): 2}
+COLS_AT = 3
 MANUAL = True
-LOADS = [("X", 0, 0), ("X", 0, 1), ("items",), ("W", 0, 0), ("W", 0, 1), ("X", 1, 0), ("X", 1, 1), ("W", 1, 0), ("X", 2, 0), ("X", 2, 1), ("W", 1, 1), ("S", 0), ("S", 1), ("W", 2, 0), ("W", 2, 1), ("S", 2), ("S", 3)]
+LOADS = [("X", 0, 0), ("X", 0, 1), ("items",), ("W", 0, 0), ("X", 1, 0), ("W", 0, 1), ("X", 1, 1), ("X", 2, 0), ("X", 2, 1), ("W", 1, 0), ("W", 1, 1), ("S", 0), ("S", 1), ("W", 2, 0), ("W", 2, 1), ("S", 2), ("S", 3)]
 PROGRAM = (
-    [("X", 0, 0), ("X", 0, 1), ("W", 0, 0), ("W", 0, 1), ("X", 1, 0), ("W", 1, 0), ("X", 1, 1), ("A", 0, 0), ("W", 1, 1), ("X", 2, 0), ("X", 2, 1), ("A", 0, 1), ("S", 0), ("W", 2, 0), ("A", 0, 2)]
-    + [("S", 1), ("W", 2, 1), ("A", 1, 0), ("S", 2), ("A", 1, 1), ("S", 3), ("B", 0, 0), ("A", 1, 2)]
-    + [("B", 0, 1), ("A", 2, 0), ("B", 0, 2), ("A", 2, 1), ("B", 0, 3), ("A", 2, 2)] + [("B", 0, b) for b in range(4, 8)] + [("width",)]
+    [("X", 0, 0), ("X", 0, 1), ("W", 0, 0), ("X", 1, 0), ("W", 0, 1), ("X", 1, 1), ("X", 2, 0), ("W", 1, 0), ("X", 2, 1), ("A", 0, 0), ("W", 1, 1), ("A", 0, 1), ("S", 0), ("W", 2, 0), ("A", 0, 2), ("S", 1), ("W", 2, 1), ("A", 1, 0), ("S", 2), ("A", 1, 1), ("S", 3)]
+    + [("B", 0, 0), ("A", 1, 2), ("B", 0, 1), ("A", 2, 0), ("B", 0, 2), ("A", 2, 1), ("B", 0, 3), ("A", 2, 2)] + [("B", 0, b) for b in range(4, 8)] + [("width",)]
     + [("B", 1, b) for b in range(8)] + [("B", 2, b) for b in range(8)]
 )
 

from contextlib import ExitStack

import concourse.mybir as mybir
from concourse.masks import make_identity

F32 = mybir.dt.float32
BF16 = mybir.dt.bfloat16
U32 = mybir.dt.uint32
U8 = mybir.dt.uint8
FP8X4 = mybir.dt.float8_e4m3fn_x4
ACT = mybir.ActivationFunctionType
ALU = mybir.AluOpType

P = 128
PACK = 4
K_PASS = P * PACK
N_TILE = 512

ITEMS, FEATURES, RANK, USERS, SLATES = 1536, 1024, 512, 1024, 1024

FLOPS = 2 * ITEMS * FEATURES * (RANK + USERS) + 2 * SLATES * ITEMS * (RANK + USERS)

GROUPS = ITEMS // K_PASS
F_PASSES = FEATURES // K_PASS
B_TILES = SLATES // P

W_COPY = {}
EXITS = {}
WARM = {("X", 0, 0): 4, ("X", 1, 0): 1, ("X", 1, 1): 2}
COLS_AT = 3
MANUAL = True
LOADS = [("X", 0, 0), ("X", 0, 1), ("items",), ("W", 0, 0), ("X", 1, 0), ("W", 0, 1), ("X", 1, 1), ("X", 2, 0), ("X", 2, 1), ("W", 1, 0), ("W", 1, 1), ("S", 0), ("S", 1), ("W", 2, 0), ("W", 2, 1), ("S", 2), ("S", 3)]
PROGRAM = (
    [("X", 0, 0), ("X", 0, 1), ("W", 0, 0), ("X", 1, 0), ("W", 0, 1), ("X", 1, 1), ("X", 2, 0), ("W", 1, 0), ("X", 2, 1), ("A", 0, 0), ("W", 1, 1), ("A", 0, 1), ("S", 0), ("W", 2, 0), ("A", 0, 2), ("S", 1), ("W", 2, 1), ("A", 1, 0), ("S", 2), ("A", 1, 1), ("S", 3)]
    + [("B", 0, 0), ("A", 1, 2), ("B", 0, 1), ("A", 2, 0), ("B", 0, 2), ("A", 2, 1), ("B", 0, 3), ("A", 2, 2)] + [("B", 0, b) for b in range(4, 8)] + [("width",)]
    + [("B", 1, b) for b in range(8)] + [("B", 2, b) for b in range(8)]
)


def tile_slate_clipped_payoff_ucb_f4_kernel(
    tc, x, cov_factor, theta, pop, cold, slates, floor_sd, alpha, ucb, width
):
    nc = tc.nc
    with ExitStack() as ctx:
        keep = ctx.enter_context(tc.tile_pool(name="keep", bufs=1))
        work = ctx.enter_context(tc.tile_pool(name="work", bufs=3))
        psum = ctx.enter_context(tc.psum_pool(name="psum", bufs=1))
        if MANUAL:
            ctx.enter_context(tc.manual_schedule())

        x_sb = [keep.tile([P, PACK, FEATURES], BF16, name="x_sb%d" % g, align_bytes=64) for g in range(GROUPS)]
        s_sb = [keep.tile([P, 2, ITEMS], BF16, name="s_sb%d" % q, align_bytes=64) for q in range(B_TILES // 2)]
        w_sb = [[keep.tile([P, PACK, N_TILE], BF16, name="w_sb%d_%d" % (c, f), align_bytes=64) for f in range(F_PASSES)] for c in range(3)]
        x_codes = [[keep.tile([P, F_PASSES, 256], U32, name="x_codes%d_%d" % (g, h), align_bytes=64) for h in range(2)] for g in range(GROUPS)]
        x_scales = [[keep.tile([P, F_PASSES, 256], U8, name="x_scales%d_%d" % (g, h), align_bytes=64) for h in range(2)] for g in range(GROUPS)]
        s_codes = [keep.tile([P, GROUPS, 256], U32, name="s_codes%d" % q, align_bytes=64) for q in range(B_TILES // 2)]
        s_scales = [keep.tile([P, GROUPS, 256], U8, name="s_scales%d" % q, align_bytes=64) for q in range(B_TILES // 2)]
        w_codes = [[keep.tile([P, N_TILE], U32, name="w_codes%d_%d" % (c, f), align_bytes=64) for f in range(F_PASSES)] for c in range(3)]
        w_scales = [[keep.tile([P, N_TILE], U8, name="w_scales%d_%d" % (c, f), align_bytes=64) for f in range(F_PASSES)] for c in range(3)]
        r_codes = [[keep.tile([P, N_TILE], U32, name="r_codes%d_%d" % (c, g), align_bytes=64) for g in range(GROUPS)] for c in range(3)]
        r_scales = [[keep.tile([P, N_TILE], U8, name="r_scales%d_%d" % (c, g), align_bytes=64) for g in range(GROUPS)] for c in range(3)]
        ident = keep.tile([P, P], F32, name="ident")
        item_rows = keep.tile([P, K_PASS], BF16, name="item_rows", align_bytes=64)
        item_cols = keep.tile([P, PACK, 2 * GROUPS], F32, name="item_cols")
        ident_bf = keep.tile([P, P], BF16, name="ident_bf")
        zeros = keep.tile([P, N_TILE], BF16, name="zeros")
        floor_bf = keep.tile([P, B_TILES], BF16, name="floor_bf")
        floor_sq = keep.tile([P, B_TILES], F32, name="floor_sq")
        alpha_bf = keep.tile([P, USERS], BF16, name="alpha_bf")
        e_sq = keep.tile([P, B_TILES], F32, name="e_sq")
        var = keep.tile([P, B_TILES], F32, name="var")
        width_col = keep.tile([P, B_TILES], F32, name="width_col")
        warm = keep.tile([P, 1], F32, name="warm")

        x_rows = x.rearrange("(g p t) k -> g p t k", p=P, t=PACK)
        s_rows = slates.rearrange("(p b) k -> p b k", b=B_TILES)
        def load_x(g, h):
            nc.sync.dma_start(out=x_sb[g][:, 2 * h : 2 * h + 2, :], in_=x_rows[g, :, 2 * h : 2 * h + 2, :])
        def load_s(q):
            nc.sync.dma_start(out=s_sb[q][:], in_=s_rows[:, 2 * q : 2 * q + 2, :])
        nc.vector.memset(zeros[:], 0.0)
        nc.gpsimd.memset(item_rows[:], 0.0)
        make_identity(nc, ident[:])
        nc.vector.tensor_copy(out=ident_bf[:], in_=ident[:])
        nc.vector.memset(warm[:], 1.0)
        nc.scalar.activation(out=warm[:], in_=warm[:], func=ACT.Sqrt)

        def load_w(c, f):
            rows = slice(f * K_PASS, (f + 1) * K_PASS)
            if c == 0:
                src = cov_factor[rows, :]
            else:
                src = theta[rows, (c - 1) * N_TILE : c * N_TILE]
            nc.sync.dma_start(out=w_sb[c][f][:], in_=src.rearrange("(p j) n -> p j n", j=PACK))

        def load_items():
            nc.sync.dma_start(out=item_rows[0:GROUPS, :], in_=cold.rearrange("(g n) -> g n", g=GROUPS))
            nc.sync.dma_start(out=item_rows[GROUPS : 2 * GROUPS, :], in_=pop.rearrange("(g n) -> g n", g=GROUPS))

        loader = {"X": load_x, "S": load_s, "W": load_w, "items": load_items}
        for load in LOADS:
            loader[load[0]](*load[1:])
        nc.sync.dma_start(out=floor_bf[:], in_=floor_sd.rearrange("(p b) -> p b", b=B_TILES))
        nc.sync.dma_start(out=alpha_bf[:], in_=alpha.partition_broadcast(P))

        used = []

        def next_bank(shape, dtype=F32):
            used.append(len(used) % 8)
            return psum.tile(shape, dtype, name="bank%d" % used[-1])

        def interleave(engine_copy, dst, src):
            engine_copy(
                out=dst.rearrange("p (c i) t -> p c t i", i=4),
                in_=src.rearrange("p t (c i) -> p c t i", i=4),
            )

        def quantize(codes, scales, grouped):
            nc.vector.quantize_mx(out=codes.bitcast(FP8X4), scales=scales, in_=grouped)

        def turn(banks, words, passes):
            for f in range(passes):
                for a in range(2):
                    for u in range(2):
                        nc.tensor.transpose(
                            banks[f][:, u, a * P : (a + 1) * P],
                            words[:, a, 256 * f + u : 256 * (f + 1) : 2],
                            ident[:],
                        )

        def x_job(g, h):
            st = {}
            def t0():
                st["banks"] = [next_bank([P, 2, 256]) for f in range(F_PASSES)]
                words = x_sb[g][:, 2 * h : 2 * h + 2, :].rearrange("p t k -> p (t k)").bitcast(F32).rearrange("p (t k) -> p t k", t=2)
                turn(st["banks"], words, F_PASSES)
            def t1():
                st["grouped"] = work.tile([P, F_PASSES * 256 * PACK], BF16, name="turned_x", align_bytes=64)
                gw = st["grouped"][:].bitcast(F32).rearrange("p (f w u) -> p f w u", f=F_PASSES, u=2)
                for f in range(F_PASSES):
                    eng = EXITS.get(("X", g, h), "SS")[f]
                    src = st["banks"][f][:].rearrange("p u w -> p w u")
                    if eng == "S":
                        nc.scalar.copy(out=gw[:, f, :, :], in_=src)
                    else:
                        nc.vector.tensor_copy(out=gw[:, f, :, :], in_=src)
            def t2():
                quantize(x_codes[g][h][:].rearrange("p f w -> p (f w)"), x_scales[g][h][:].rearrange("p f w -> p (f w)"), st["grouped"][:])
            return [t0, t1, t2]

        def s_job(q):
            st = {}
            def t0():
                st["banks"] = [next_bank([P, 2, 256]) for f in range(GROUPS)]
                words = s_sb[q][:].rearrange("p t k -> p (t k)").bitcast(F32).rearrange("p (t k) -> p t k", t=2)
                turn(st["banks"], words, GROUPS)
            def t1():
                st["grouped"] = work.tile([P, GROUPS * 256 * PACK], BF16, name="turned_s", align_bytes=64)
                gw = st["grouped"][:].bitcast(F32).rearrange("p (f w u) -> p f w u", f=GROUPS, u=2)
                for f in range(GROUPS):
                    eng = EXITS.get(("S", q), "SSS")[f]
                    src = st["banks"][f][:].rearrange("p u w -> p w u")
                    if eng == "S":
                        nc.scalar.copy(out=gw[:, f, :, :], in_=src)
                    else:
                        nc.vector.tensor_copy(out=gw[:, f, :, :], in_=src)
            def t2():
                codes = s_codes[q][:].rearrange("p f w -> p (f w)")
                scales = s_scales[q][:].rearrange("p f w -> p (f w)")
                quantize(codes[:, :512], scales[:, :512], st["grouped"][:, :2048])
                quantize(codes[:, 512:], scales[:, 512:], st["grouped"][:, 2048:])
            return [t0, t1, t2]

        def w_job(c, f):
            st = {}
            def t0():
                src = w_sb[c][f][:]
                st["grouped"] = work.tile([P, N_TILE, PACK], BF16, name="grouped_w", align_bytes=64)
                copy = nc.scalar.copy if W_COPY.get((c, f), "V") == "S" else nc.vector.tensor_copy
                interleave(copy, st["grouped"][:], src)
            def t1():
                quantize(w_codes[c][f][:], w_scales[c][f][:], st["grouped"][:].rearrange("p n t -> p (n t)"))
            return [t0, t1]

        def a_job(c, g):
            st = {}
            def t0():
                st["banks"] = []
                for t in range(PACK):
                    bank = next_bank([P, N_TILE])
                    for f in range(F_PASSES):
                        cols = slice((t % 2) * P, (t % 2 + 1) * P)
                        nc.tensor.matmul_mx(
                            out=bank[:],
                            lhsT=x_codes[g][t // 2][:, f, cols].bitcast(FP8X4),
                            lhsT_scale=x_scales[g][t // 2][:, f, cols],
                            rhs=w_codes[c][f][:].bitcast(FP8X4),
                            rhs_scale=w_scales[c][f][:],
                            start=(f == 0),
                            stop=(f == F_PASSES - 1),
                        )
                    st["banks"].append(bank)
            def t1():
                st["rows"] = work.tile([P, PACK, N_TILE], BF16, name="rows", align_bytes=64, bufs=4)
                for t in range(PACK):
                    bank = st["banks"][t]
                    if c == 0:
                        if EXITS.get(("A", c, g), "SSSS")[t] == "S":
                            nc.scalar.activation(out=st["rows"][:, t, :], in_=bank[:], func=ACT.Copy, scale=item_cols[:, t, g : g + 1])
                        else:
                            nc.vector.tensor_scalar(out=st["rows"][:, t, :], in0=bank[:], scalar1=item_cols[:, t, g : g + 1], scalar2=None, op0=ALU.mult)
                    else:
                        if EXITS.get(("A", c, g), "SSSS")[t] == "S":
                            nc.scalar.activation(out=st["rows"][:, t, :], in_=bank[:], func=ACT.Relu, bias=item_cols[:, t, GROUPS + g : GROUPS + g + 1])
                        else:
                            nc.vector.tensor_scalar(out=st["rows"][:, t, :], in0=bank[:], scalar1=item_cols[:, t, GROUPS + g : GROUPS + g + 1], scalar2=0.0, op0=ALU.add, op1=ALU.max)
            def t2():
                st["grouped"] = work.tile([P, N_TILE, PACK], BF16, name="grouped_r", align_bytes=64)
                interleave(nc.vector.tensor_copy, st["grouped"][:], st["rows"][:])
            def t3():
                quantize(r_codes[c][g][:], r_scales[c][g][:], st["grouped"][:].rearrange("p n t -> p (n t)"))
            return [t0, t1, t2, t3]

        def b_job(c, b):
            st = {}
            parts = [slice(0, N_TILE)] if (c, b) != (2, B_TILES - 1) else [slice(0, N_TILE // 2), slice(N_TILE // 2, N_TILE)]
            def t0():
                st["banks"] = []
                cols = slice((b % 2) * P, (b % 2 + 1) * P)
                for part in parts:
                    bank = next_bank([P, part.stop - part.start])
                    for g in range(GROUPS):
                        nc.tensor.matmul_mx(
                            out=bank[:],
                            lhsT=s_codes[b // 2][:, g, cols].bitcast(FP8X4),
                            lhsT_scale=s_scales[b // 2][:, g, cols],
                            rhs=r_codes[c][g][:, part].bitcast(FP8X4),
                            rhs_scale=r_scales[c][g][:, part],
                            start=(g == 0),
                            stop=(g == GROUPS - 1),
                        )
                    st["banks"].append(bank)
            def t1():
                if c == 0:
                    junk = work.tile([P, N_TILE], F32, name="junk", bufs=1)
                    nc.scalar.activation(out=junk[:], in_=st["banks"][0][:], func=ACT.Square, accum_out=e_sq[:, b : b + 1])
                else:
                    for bank, part in zip(st["banks"], parts):
                        users = slice((c - 1) * N_TILE + part.start, (c - 1) * N_TILE + part.stop)
                        res = work.tile([P, part.stop - part.start], F32, name="res", bufs=8)
                        nc.vector.scalar_tensor_tensor(
                            out=res[:], in0=alpha_bf[:, users], scalar=width_col[:, b : b + 1], in1=bank[:], op0=ALU.mult, op1=ALU.add,
                        )
                        nc.sync.dma_start(out=ucb.rearrange("(p b) n -> p b n", b=B_TILES)[:, b, users], in_=res[:])
            return [t0, t1]

        def width_job():
            def t0():
                nc.vector.tensor_tensor(out=floor_sq[:], in0=floor_bf[:], in1=floor_bf[:], op=ALU.mult)
                nc.vector.scalar_tensor_tensor(out=var[:], in0=e_sq[:], scalar=1.0 / RANK, in1=floor_sq[:], op0=ALU.mult, op1=ALU.add)
                nc.scalar.activation(out=width_col[:], in_=var[:], func=ACT.Sqrt)
                nc.sync.dma_start(out=width.rearrange("(p b) -> p b", b=B_TILES), in_=width_col[:])
            return [t0]

        def item_columns():
            bank = next_bank([P, PACK, P], BF16)
            for t in range(PACK):
                nc.tensor.transpose(bank[:, t, :], item_rows[:, t::PACK], ident_bf[:])
            nc.vector.tensor_copy(out=item_cols[:], in_=bank[:, :, 0 : 2 * GROUPS])

        def warm_up(n):
            if n:
                bank = next_bank([P, N_TILE])
                for i in range(n):
                    nc.tensor.matmul(bank[:], lhsT=zeros[:, :P], rhs=zeros[:], start=True, stop=True)

        make = {"X": x_job, "S": s_job, "W": w_job, "A": a_job, "B": b_job, "width": width_job}
        jobs = [make[step[0]](*step[1:]) for step in PROGRAM]
        for i in range(len(jobs) + 3):
            for s in (3, 2, 1, 0):
                if 0 <= i - s < len(jobs) and s < len(jobs[i - s]):
                    if s == 0:
                        warm_up(WARM.get(PROGRAM[i], 0))
                    if s == 0 and i == COLS_AT:
                        item_columns()
                    jobs[i - s][s]()
